import numpy as np
CORES = [7,15,23,31,39,47,55,63,71,79,87,95,103,111,119,127,135,143,151,159,167,175,183,191,199,207,215,223,231,239,247,255,263,271,279,287,295,303,311,319,327,335,343,351,359,367,375,383,391,399,407,415,423,431,439,447,455,463,471,479,487,495,503,511]
N = 64
ROUNDS = 8
ROOTS = [37,2,60,25,11,48,30,55]
def setup_inputs(rng):
    return {"x": rng.standard_normal((N, ROUNDS, 128, 64), dtype=np.float32)}
def reference(x):
    g = np.stack([x[ROOTS[k]][k] for k in range(ROUNDS)])
    return {"y": np.broadcast_to(g, (N,) + g.shape)}

@@ -1,0 +1,133 @@
+import concourse.bass as bass
+
+ROUNDS, NSLOT, NR = 8, 3, 64
+SCRATCH = {"slot": ("dram", [NSLOT, 128, 64], "float32")}
+SEMAPHORES = (["arr%d" % k for k in range(ROUNDS)] + ["cr%d" % k for k in range(ROUNDS)]
+              + ["snt%d" % k for k in range(ROUNDS)] + ["st%d" % k for k in range(ROUNDS)] + ["ld", "sig"])
+
+LONG = (5,)
+HELP = {0: (4, 6, 8, 10), 1: (1, 3, 13, 15)}
+
+
+def trees(roots):
+    par = []
+    seen = {0: 0, 1: 0}
+    for k, root in enumerate(roots):
+        h, c = root // 16, root % 16
+        p = c % 2
+        b = HELP[p][seen[p]]
+        seen[p] += 1
+        up = [None] * NR
+        if k in LONG:
+            hops = [(h, h ^ 1), (h ^ 1, 3 - (h ^ 1)), (3 - (h ^ 1), 3 - h)]
+        else:
+            hops = [(h, h ^ 1), (h, 3 - h), (3 - h, (3 - h) ^ 1)]
+        for a, d in hops:
+            up[d * 16 + c] = a * 16 + c
+        for hh in range(4):
+            rest = [q for q in range(p, 16, 2) if q != c and q != b]
+            up[hh * 16 + b] = hh * 16 + c
+            for q in rest[:2]:
+                up[hh * 16 + q] = hh * 16 + c
+            for q in rest[2:]:
+                up[hh * 16 + q] = hh * 16 + b
+            for q in range(p, 16, 2):
+                up[hh * 16 + (q ^ 1)] = hh * 16 + q
+        par.append(up)
+    return par
+
+
+def schedule(roots):
+    par = trees(roots)
+    prev = [k - NSLOT if k >= NSLOT else None for k in range(ROUNDS)]
+    nxt = [k + NSLOT if k + NSLOT < ROUNDS else None for k in range(ROUNDS)]
+    kids = [[[c for c in range(NR) if par[k][c] == r] for r in range(NR)] for k in range(ROUNDS)]
+    land = [[None] * NR for k in range(ROUNDS)]
+    cred = [[None] * NR for k in range(ROUNDS)]
+    got = [[False] * NR for k in range(ROUNDS)]
+    sent = [[False] * NR for k in range(ROUNDS)]
+    freed = [[False] * NR for k in range(ROUNDS)]
+    ops = [[] for r in range(NR)]
+    step = 0
+    while not all(all(f) for f in freed):
+        new = []
+        for r in range(NR):
+            moved = True
+            while moved:
+                moved = False
+                for k in range(ROUNDS):
+                    if not got[k][r]:
+                        if roots[k] == r:
+                            if prev[k] is None or freed[prev[k]][r]:
+                                ops[r].append(("load", k))
+                                got[k][r] = moved = True
+                        elif land[k][r] is not None and land[k][r] <= step:
+                            ops[r].append(("recv", k))
+                            got[k][r] = moved = True
+                    if got[k][r] and not sent[k][r]:
+                        ch = kids[k][r]
+                        if prev[k] is None or all(cred[k][c] is not None and cred[k][c] <= step for c in ch):
+                            if ch:
+                                ops[r].append(("fwd", k, tuple(ch), prev[k] is not None))
+                                for c in ch:
+                                    new.append((land, k, c))
+                            sent[k][r] = moved = True
+                    if sent[k][r] and not freed[k][r]:
+                        n = nxt[k]
+                        ops[r].append(("free", k, bool(kids[k][r]), None if n is None or roots[n] == r else (n, par[n][r])))
+                        if n is not None and roots[n] != r:
+                            new.append((cred, n, r))
+                        freed[k][r] = moved = True
+        step += 1
+        for tab, k, c in new:
+            tab[k][c] = step
+        assert step < 200
+    return ops, step
+
+
+CACHE = {}
+
+
+def rank_program(g, core, T, topo):
+    rank = T.rank_of(core)
+    if rank is None:
+        return
+    roots = list(T.tables["ROOTS"])
+    if "ops" not in CACHE:
+        CACHE["ops"] = schedule(roots)[0]
+    s = T.sem
+    arr = [s.arr0, s.arr1, s.arr2, s.arr3, s.arr4, s.arr5, s.arr6, s.arr7]
+    cr = [s.cr0, s.cr1, s.cr2, s.cr3, s.cr4, s.cr5, s.cr6, s.cr7]
+    snt = [s.snt0, s.snt1, s.snt2, s.snt3, s.snt4, s.snt5, s.snt6, s.snt7]
+    st = [s.st0, s.st1, s.st2, s.st3, s.st4, s.st5, s.st6, s.st7]
+    nsig = 0
+    for op in CACHE["ops"][rank]:
+        k = op[1]
+        buf = T.slot[k % NSLOT]
+        if op[0] == "load":
+            g.dma_start(T.y[k], T.x[k]).then_inc(st[k], 16)
+            g.dma_start(buf, T.x[k]).then_inc(s.ld, 16)
+            g.wait_ge(s.ld, 16)
+        elif op[0] == "recv":
+            g.wait_ge(arr[k], 8)
+            g.dma_start(T.y[k], buf).then_inc(st[k], 16)
+        elif op[0] == "fwd":
+            if op[3]:
+                g.wait_ge(cr[k], len(op[2]))
+            ids = []
+            for c in op[2]:
+                rid, pid = topo.addr(T.cores[c], core)
+                ids.append(bass.DstId(rid=rid, pnc=pid))
+            g.remote_dma_fused([bass.RemoteDMATransfer(dst_ids=ids, dma_engine_mask=0xFF, remote_sem=arr[k],
+                                                       srcs=[buf], dsts=[buf] * len(ids))], local_sem=snt[k])
+        else:
+            g.wait_ge(st[k], 16)
+            if op[2]:
+                g.wait_ge(snt[k], 8)
+            if op[3] is not None:
+                n, up = op[3]
+                rid, pid = topo.addr(T.cores[up], core)
+                g.remote_sem_update(cr[n], s.sig, pid, rid, 0x01)
+                nsig += 1
+    if nsig:
+        g.wait_ge(s.sig, nsig)

@@ -2,87 +2,167 @@ import concourse.bass as bass
 
 ROUNDS, NSLOT, NR = 8, 3, 64
 SCRATCH = {"slot": ("dram", [NSLOT, 128, 64], "float32")}
-SEMAPHORES = (["arr%d" % k for k in range(ROUNDS)] + ["cr%d" % k for k in range(ROUNDS)]
-              + ["snt%d" % k for k in range(ROUNDS)] + ["st%d" % k for k in range(ROUNDS)] + ["ld", "sig"])
+SEMAPHORES = (["arr%d" % k for k in range(ROUNDS)]
+              + ["cr%d" % k for k in range(ROUNDS)]
+              + ["snt%d" % k for k in range(ROUNDS)]
+              + ["st%d" % k for k in range(ROUNDS)]
+              + ["ld", "sig"])
 
-LONG = (5,)
-HELP = {0: (4, 6, 8, 10), 1: (1, 3, 13, 15)}
+LONG = 5
+LAST = 7
+
+FEED = [
+    "45555-444445554554455-544545454444555-544443454545455-4545454554",
+    "24-223333223233333-223232322323223-222222333333223-2333223232233",
+    "cccdcdddcdcd-cddcddccdcdcddc-ccdcdcddddccccd-ccdcddccd4cdddd-ccd",
+    "889999889-998988898988899-983889888989999-888998898998989-898989",
+    "abaabbaabab-aba1bbabaaabbab-abababababbaabb-abbaaaabbbababb-aaba",
+    "-001110010010101-001101110010101-001110101011010-001110001110011",
+    "efffffeeeeefef-ef6feefeeffefff-eefeeeffffeffef-effefeeefefeeff-e",
+    "6766677-676776677667777-676766766766777-66776767f767667-66667767",
+]
+STEP = [
+    "7555547777755575455441455454545533111013333231317575517575757557",
+    "1501122221121222771337373733737357355555577777753713777337373377",
+    "3334344434341344455445454554344557577775555715571221123122220112",
+    "7722227721227277212122211012222155525222215552257373373732737373",
+    "2122112212102123227277722721727275757557755375575553335353315535",
+    "3667776676676767233773777337373712255525252552520115551115551155",
+    "5777775555575715525115115515550137333777737737137757555757557735",
+    "5355533153533553677666637676776773773331773373732171771077771171",
+]
 
 
-def trees(roots):
-    par = []
-    seen = {0: 0, 1: 0}
-    for k, root in enumerate(roots):
-        h, c = root // 16, root % 16
-        p = c % 2
-        b = HELP[p][seen[p]]
-        seen[p] += 1
-        up = [None] * NR
-        if k in LONG:
-            hops = [(h, h ^ 1), (h ^ 1, 3 - (h ^ 1)), (3 - (h ^ 1), 3 - h)]
+def hops_of(k, h):
+    if k == LONG:
+        return [(h, h ^ 1), (h ^ 1, 3 - (h ^ 1)), (3 - (h ^ 1), 3 - h)]
+    return [(h, h ^ 1), (h, 3 - h), (3 - h, (3 - h) ^ 1)]
+
+
+def fewest_points(windows):
+    groups = []
+    for lo, hi, tag in sorted(windows, key=lambda w: (w[1], w[0], w[2])):
+        if groups and lo <= groups[-1][1]:
+            groups[-1][0] = max(groups[-1][0], lo)
+            groups[-1][2].append(tag)
         else:
-            hops = [(h, h ^ 1), (h, 3 - h), (3 - h, (3 - h) ^ 1)]
-        for a, d in hops:
-            up[d * 16 + c] = a * 16 + c
-        for hh in range(4):
-            rest = [q for q in range(p, 16, 2) if q != c and q != b]
-            up[hh * 16 + b] = hh * 16 + c
-            for q in rest[:2]:
-                up[hh * 16 + q] = hh * 16 + c
-            for q in rest[2:]:
-                up[hh * 16 + q] = hh * 16 + b
-            for q in range(p, 16, 2):
-                up[hh * 16 + (q ^ 1)] = hh * 16 + q
-        par.append(up)
-    return par
+            groups.append([lo, hi, [tag]])
+    return groups
 
 
-def schedule(roots):
-    par = trees(roots)
-    prev = [k - NSLOT if k >= NSLOT else None for k in range(ROUNDS)]
-    nxt = [k + NSLOT if k + NSLOT < ROUNDS else None for k in range(ROUNDS)]
-    kids = [[[c for c in range(NR) if par[k][c] == r] for r in range(NR)] for k in range(ROUNDS)]
-    land = [[None] * NR for k in range(ROUNDS)]
-    cred = [[None] * NR for k in range(ROUNDS)]
-    got = [[False] * NR for k in range(ROUNDS)]
-    sent = [[False] * NR for k in range(ROUNDS)]
-    freed = [[False] * NR for k in range(ROUNDS)]
-    ops = [[] for r in range(NR)]
-    step = 0
-    while not all(all(f) for f in freed):
-        new = []
+def chip_plan(stays):
+    land = [s[0] for s in stays]
+    hold = [s[1] for s in stays]
+    own = [s[2] for s in stays]
+    start = [land[k] + (2 if own[k] else 0) for k in range(ROUNDS)]
+    by_land = sorted(range(ROUNDS), key=lambda k: (land[k], k))
+    best = [None]
+
+    def colour(free, batch_of, cap):
+        seq = sorted(range(ROUNDS), key=lambda k: (start[k], free[k]))
+        found = [None]
+        slot = [None] * ROUNDS
+        last = [None] * NSLOT
+
+        def place(i, windows):
+            n = len(fewest_points(windows))
+            if n >= cap or (found[0] is not None and n >= found[0][0]):
+                return
+            if i == ROUNDS:
+                found[0] = (n, list(slot), list(windows))
+                return
+            k = seq[i]
+            for s in range(NSLOT):
+                p = last[s]
+                if p is not None and free[p] + 2 > start[k]:
+                    continue
+                group = batch_of[k]
+                if any(j != k and slot[j] is not None and ((slot[j] < s) != (j < k) or slot[j] == s) for j in group):
+                    continue
+                if len(group) == NSLOT and s != sorted(group).index(k):
+                    continue
+                slot[k], last[s] = s, k
+                place(i + 1, windows + ([(free[p], land[k] - 2, k)] if p is not None and not own[k] else []))
+                slot[k], last[s] = None, p
+        place(0, [])
+        return found[0]
+
+    def split(i, batches):
+        if best[0] is not None and len(batches) + 2 >= best[0][0]:
+            return
+        if i == ROUNDS:
+            free = list(hold)
+            batch_of = {}
+            for b in batches:
+                for k in b:
+                    free[k] = max(hold[k], max(land[j] for j in b))
+                    batch_of[k] = b
+            c = colour(free, batch_of, 99 if best[0] is None else best[0][0] - len(batches))
+            if c is not None:
+                best[0] = (len(batches) + c[0], [sorted(b) for b in batches], c[1], c[2])
+            return
+        k = by_land[i]
+        for b in batches:
+            t = sorted(b + [k])
+            if len(t) <= NSLOT and (len(t) < 3 or t[1] - t[0] == t[2] - t[1]):
+                b.append(k)
+                split(i + 1, batches)
+                b.pop()
+        batches.append([k])
+        split(i + 1, batches)
+        batches.pop()
+
+    split(0, [])
+    assert best[0] is not None, "the timetable needs a fourth slot"
+    total, batches, slot, windows = best[0]
+    return slot, batches, [(g[0], sorted(g[2])) for g in fewest_points(windows)]
+
+
+def plan(roots):
+    up = []
+    for k, root in enumerate(roots):
+        c = root % 16
+        row = [None if FEED[k][r] == "-" else (r // 16) * 16 + int(FEED[k][r], 16) for r in range(NR)]
+        for a, d in hops_of(k, root // 16):
+            row[d * 16 + c] = a * 16 + c
+        up.append(row)
+    land = [[int(ch) for ch in STEP[k]] for k in range(ROUNDS)]
+    kids = [[[q for q in range(NR) if up[k][q] == r] for r in range(NR)] for k in range(ROUNDS)]
+    call = [[None] * NR for k in range(ROUNDS)]
+    for k in range(ROUNDS):
+        assert [r for r in range(NR) if up[k][r] is None] == [roots[k]]
         for r in range(NR):
-            moved = True
-            while moved:
-                moved = False
-                for k in range(ROUNDS):
-                    if not got[k][r]:
-                        if roots[k] == r:
-                            if prev[k] is None or freed[prev[k]][r]:
-                                ops[r].append(("load", k))
-                                got[k][r] = moved = True
-                        elif land[k][r] is not None and land[k][r] <= step:
-                            ops[r].append(("recv", k))
-                            got[k][r] = moved = True
-                    if got[k][r] and not sent[k][r]:
-                        ch = kids[k][r]
-                        if prev[k] is None or all(cred[k][c] is not None and cred[k][c] <= step for c in ch):
-                            if ch:
-                                ops[r].append(("fwd", k, tuple(ch), prev[k] is not None))
-                                for c in ch:
-                                    new.append((land, k, c))
-                            sent[k][r] = moved = True
-                    if sent[k][r] and not freed[k][r]:
-                        n = nxt[k]
-                        ops[r].append(("free", k, bool(kids[k][r]), None if n is None or roots[n] == r else (n, par[n][r])))
-                        if n is not None and roots[n] != r:
-                            new.append((cred, n, r))
-                        freed[k][r] = moved = True
-        step += 1
-        for tab, k, c in new:
-            tab[k][c] = step
-        assert step < 200
-    return ops, step
+            if kids[k][r]:
+                steps = sorted(set(land[k][q] for q in kids[k][r]))
+                assert len(steps) == 1 and land[k][r] < steps[0] <= LAST and len(kids[k][r]) <= 8
+                call[k][r] = steps[0]
+    slot, credited, ops = [], [], []
+    for r in range(NR):
+        assert sum(len(kids[k][r]) for k in range(ROUNDS)) <= 8
+        stays = [(land[k][r], call[k][r] if kids[k][r] else land[k][r], roots[k] == r) for k in range(ROUNDS)]
+        where, batches, credits = chip_plan(stays)
+        slot.append(where)
+        credited.append(set(k for step, ks in credits for k in ks))
+        before = {}
+        for s in range(NSLOT):
+            seq = sorted((k for k in range(ROUNDS) if where[k] == s), key=lambda k: land[k][r])
+            for a, b in zip(seq, seq[1:]):
+                before[b] = a
+        o = []
+        for k in range(ROUNDS):
+            if roots[k] == r:
+                o.append((land[k][r], 3, "load", (k, before.get(k))))
+            else:
+                o.append((land[k][r], 0, "recv", k))
+            if kids[k][r]:
+                o.append((call[k][r] - 1, 4 if roots[k] == r else 1, "send", k))
+        for i, b in enumerate(batches):
+            o.append((max(land[k][r] for k in b), 5 if any(roots[k] == r for k in b) else 2, "store", (i, b)))
+        for step, ks in credits:
+            o.append((step, 6, "credit", [(k, before[k]) for k in ks]))
+        o.sort()
+        ops.append((o, dict((k, i) for i, b in enumerate(batches) for k in b)))
+    return up, kids, slot, credited, ops
 
 
 CACHE = {}
@@ -92,42 +172,64 @@ def rank_program(g, core, T, topo):
     rank = T.rank_of(core)
     if rank is None:
         return
-    roots = list(T.tables["ROOTS"])
-    if "ops" not in CACHE:
-        CACHE["ops"] = schedule(roots)[0]
+    if "plan" not in CACHE:
+        CACHE["plan"] = plan(list(T.tables["ROOTS"]))
+    up, kids, slot, credited, ops = CACHE["plan"]
     s = T.sem
     arr = [s.arr0, s.arr1, s.arr2, s.arr3, s.arr4, s.arr5, s.arr6, s.arr7]
     cr = [s.cr0, s.cr1, s.cr2, s.cr3, s.cr4, s.cr5, s.cr6, s.cr7]
     snt = [s.snt0, s.snt1, s.snt2, s.snt3, s.snt4, s.snt5, s.snt6, s.snt7]
     st = [s.st0, s.st1, s.st2, s.st3, s.st4, s.st5, s.st6, s.st7]
-    nsig = 0
-    for op in CACHE["ops"][rank]:
-        k = op[1]
-        buf = T.slot[k % NSLOT]
-        if op[0] == "load":
-            g.dma_start(T.y[k], T.x[k]).then_inc(st[k], 16)
-            g.dma_start(buf, T.x[k]).then_inc(s.ld, 16)
+    todo, batch_of = ops[rank]
+    open_stores, open_calls = set(), set()
+
+    def dst(r):
+        rid, pid = topo.addr(T.cores[r], core)
+        return bass.DstId(rid=rid, pnc=pid)
+
+    def release(k):
+        if batch_of[k] in open_stores:
+            g.wait_ge(st[batch_of[k]], 16)
+            open_stores.discard(batch_of[k])
+        if k in open_calls:
+            g.wait_ge(snt[k], 8)
+            open_calls.discard(k)
+
+    signals = 0
+    for step, order, what, arg in todo:
+        if what == "recv":
+            g.wait_ge(arr[arg], 8)
+        elif what == "load":
+            k, old = arg
+            if old is not None:
+                release(old)
+            g.dma_start(T.slot[slot[rank][k]], T.x[k]).then_inc(s.ld, 16)
             g.wait_ge(s.ld, 16)
-        elif op[0] == "recv":
-            g.wait_ge(arr[k], 8)
-            g.dma_start(T.y[k], buf).then_inc(st[k], 16)
-        elif op[0] == "fwd":
-            if op[3]:
-                g.wait_ge(cr[k], len(op[2]))
-            ids = []
-            for c in op[2]:
-                rid, pid = topo.addr(T.cores[c], core)
-                ids.append(bass.DstId(rid=rid, pnc=pid))
-            g.remote_dma_fused([bass.RemoteDMATransfer(dst_ids=ids, dma_engine_mask=0xFF, remote_sem=arr[k],
-                                                       srcs=[buf], dsts=[buf] * len(ids))], local_sem=snt[k])
+        elif what == "send":
+            k = arg
+            need = sum(1 for q in kids[k][rank] if k in credited[q])
+            if need:
+                g.wait_ge(cr[k], need)
+            g.remote_dma_fused([bass.RemoteDMATransfer(
+                dst_ids=[dst(q) for q in kids[k][rank]], dma_engine_mask=0xFF, remote_sem=arr[k],
+                srcs=[T.slot[slot[rank][k]]], dsts=[T.slot[slot[q][k]] for q in kids[k][rank]])], local_sem=snt[k])
+            open_calls.add(k)
+        elif what == "store":
+            i, ks = arg
+            a, b = slot[rank][ks[0]], slot[rank][ks[-1]]
+            if len(ks) == 1:
+                g.dma_start(T.y[ks[0]], T.slot[a]).then_inc(st[i], 16)
+            else:
+                g.dma_start(T.y[ks[0]:ks[-1] + 1:ks[1] - ks[0]],
+                            T.slot[a:b + 1:(b - a) // (len(ks) - 1)]).then_inc(st[i], 16)
+            open_stores.add(i)
         else:
-            g.wait_ge(st[k], 16)
-            if op[2]:
-                g.wait_ge(snt[k], 8)
-            if op[3] is not None:
-                n, up = op[3]
-                rid, pid = topo.addr(T.cores[up], core)
-                g.remote_sem_update(cr[n], s.sig, pid, rid, 0x01)
-                nsig += 1
-    if nsig:
-        g.wait_ge(s.sig, nsig)
+            for k, old in arg:
+                release(old)
+            g.remote_dma_fused([bass.RemoteDMATransfer(dst_ids=[dst(up[k][rank])], dma_engine_mask=1 << i, remote_sem=cr[k])
+                                for i, (k, old) in enumerate(arg)], local_sem=s.sig)
+            signals += len(arg)
+    for k in range(ROUNDS):
+        release(k)
+    if signals:
+        g.wait_ge(s.sig, signals)

import concourse.bass as bass

ROUNDS, NSLOT, NR = 8, 3, 64
SCRATCH = {"slot": ("dram", [NSLOT, 128, 64], "float32")}
SEMAPHORES = (["arr%d" % k for k in range(ROUNDS)]
              + ["cr%d" % k for k in range(ROUNDS)]
              + ["snt%d" % k for k in range(ROUNDS)]
              + ["st%d" % k for k in range(ROUNDS)]
              + ["ld", "sig"])

LONG = 5
LAST = 7

FEED = [
    "45555-444445554554455-544545454444555-544443454545455-4545454554",
    "24-223333223233333-223232322323223-222222333333223-2333223232233",
    "cccdcdddcdcd-cddcddccdcdcddc-ccdcdcddddccccd-ccdcddccd4cdddd-ccd",
    "889999889-998988898988899-983889888989999-888998898998989-898989",
    "abaabbaabab-aba1bbabaaabbab-abababababbaabb-abbaaaabbbababb-aaba",
    "-001110010010101-001101110010101-001110101011010-001110001110011",
    "efffffeeeeefef-ef6feefeeffefff-eefeeeffffeffef-effefeeefefeeff-e",
    "6766677-676776677667777-676766766766777-66776767f767667-66667767",
]
STEP = [
    "7555547777755575455441455454545533111013333231317575517575757557",
    "1501122221121222771337373733737357355555577777753713777337373377",
    "3334344434341344455445454554344557577775555715571221123122220112",
    "7722227721227277212122211012222155525222215552257373373732737373",
    "2122112212102123227277722721727275757557755375575553335353315535",
    "3667776676676767233773777337373712255525252552520115551115551155",
    "5777775555575715525115115515550137333777737737137757555757557735",
    "5355533153533553677666637676776773773331773373732171771077771171",
]


def hops_of(k, h):
    if k == LONG:
        return [(h, h ^ 1), (h ^ 1, 3 - (h ^ 1)), (3 - (h ^ 1), 3 - h)]
    return [(h, h ^ 1), (h, 3 - h), (3 - h, (3 - h) ^ 1)]


def fewest_points(windows):
    groups = []
    for lo, hi, tag in sorted(windows, key=lambda w: (w[1], w[0], w[2])):
        if groups and lo <= groups[-1][1]:
            groups[-1][0] = max(groups[-1][0], lo)
            groups[-1][2].append(tag)
        else:
            groups.append([lo, hi, [tag]])
    return groups


def chip_plan(stays):
    land = [s[0] for s in stays]
    hold = [s[1] for s in stays]
    own = [s[2] for s in stays]
    start = [land[k] + (2 if own[k] else 0) for k in range(ROUNDS)]
    by_land = sorted(range(ROUNDS), key=lambda k: (land[k], k))
    best = [None]

    def colour(free, batch_of, cap):
        seq = sorted(range(ROUNDS), key=lambda k: (start[k], free[k]))
        found = [None]
        slot = [None] * ROUNDS
        last = [None] * NSLOT

        def place(i, windows):
            n = len(fewest_points(windows))
            if n >= cap or (found[0] is not None and n >= found[0][0]):
                return
            if i == ROUNDS:
                found[0] = (n, list(slot), list(windows))
                return
            k = seq[i]
            for s in range(NSLOT):
                p = last[s]
                if p is not None and free[p] + 2 > start[k]:
                    continue
                group = batch_of[k]
                if any(j != k and slot[j] is not None and ((slot[j] < s) != (j < k) or slot[j] == s) for j in group):
                    continue
                if len(group) == NSLOT and s != sorted(group).index(k):
                    continue
                slot[k], last[s] = s, k
                place(i + 1, windows + ([(free[p], land[k] - 2, k)] if p is not None and not own[k] else []))
                slot[k], last[s] = None, p
        place(0, [])
        return found[0]

    def split(i, batches):
        if best[0] is not None and len(batches) + 2 >= best[0][0]:
            return
        if i == ROUNDS:
            free = list(hold)
            batch_of = {}
            for b in batches:
                for k in b:
                    free[k] = max(hold[k], max(land[j] for j in b))
                    batch_of[k] = b
            c = colour(free, batch_of, 99 if best[0] is None else best[0][0] - len(batches))
            if c is not None:
                best[0] = (len(batches) + c[0], [sorted(b) for b in batches], c[1], c[2])
            return
        k = by_land[i]
        for b in batches:
            t = sorted(b + [k])
            if len(t) <= NSLOT and (len(t) < 3 or t[1] - t[0] == t[2] - t[1]):
                b.append(k)
                split(i + 1, batches)
                b.pop()
        batches.append([k])
        split(i + 1, batches)
        batches.pop()

    split(0, [])
    assert best[0] is not None, "the timetable needs a fourth slot"
    total, batches, slot, windows = best[0]
    return slot, batches, [(g[0], sorted(g[2])) for g in fewest_points(windows)]


def plan(roots):
    up = []
    for k, root in enumerate(roots):
        c = root % 16
        row = [None if FEED[k][r] == "-" else (r // 16) * 16 + int(FEED[k][r], 16) for r in range(NR)]
        for a, d in hops_of(k, root // 16):
            row[d * 16 + c] = a * 16 + c
        up.append(row)
    land = [[int(ch) for ch in STEP[k]] for k in range(ROUNDS)]
    kids = [[[q for q in range(NR) if up[k][q] == r] for r in range(NR)] for k in range(ROUNDS)]
    call = [[None] * NR for k in range(ROUNDS)]
    for k in range(ROUNDS):
        assert [r for r in range(NR) if up[k][r] is None] == [roots[k]]
        for r in range(NR):
            if kids[k][r]:
                steps = sorted(set(land[k][q] for q in kids[k][r]))
                assert len(steps) == 1 and land[k][r] < steps[0] <= LAST and len(kids[k][r]) <= 8
                call[k][r] = steps[0]
    slot, credited, ops = [], [], []
    for r in range(NR):
        assert sum(len(kids[k][r]) for k in range(ROUNDS)) <= 8
        stays = [(land[k][r], call[k][r] if kids[k][r] else land[k][r], roots[k] == r) for k in range(ROUNDS)]
        where, batches, credits = chip_plan(stays)
        slot.append(where)
        credited.append(set(k for step, ks in credits for k in ks))
        before = {}
        for s in range(NSLOT):
            seq = sorted((k for k in range(ROUNDS) if where[k] == s), key=lambda k: land[k][r])
            for a, b in zip(seq, seq[1:]):
                before[b] = a
        o = []
        for k in range(ROUNDS):
            if roots[k] == r:
                o.append((land[k][r], 3, "load", (k, before.get(k))))
            else:
                o.append((land[k][r], 0, "recv", k))
            if kids[k][r]:
                o.append((call[k][r] - 1, 4 if roots[k] == r else 1, "send", k))
        for i, b in enumerate(batches):
            o.append((max(land[k][r] for k in b), 5 if any(roots[k] == r for k in b) else 2, "store", (i, b)))
        for step, ks in credits:
            o.append((step, 6, "credit", [(k, before[k]) for k in ks]))
        o.sort()
        ops.append((o, dict((k, i) for i, b in enumerate(batches) for k in b)))
    return up, kids, slot, credited, ops


CACHE = {}


def rank_program(g, core, T, topo):
    rank = T.rank_of(core)
    if rank is None:
        return
    if "plan" not in CACHE:
        CACHE["plan"] = plan(list(T.tables["ROOTS"]))
    up, kids, slot, credited, ops = CACHE["plan"]
    s = T.sem
    arr = [s.arr0, s.arr1, s.arr2, s.arr3, s.arr4, s.arr5, s.arr6, s.arr7]
    cr = [s.cr0, s.cr1, s.cr2, s.cr3, s.cr4, s.cr5, s.cr6, s.cr7]
    snt = [s.snt0, s.snt1, s.snt2, s.snt3, s.snt4, s.snt5, s.snt6, s.snt7]
    st = [s.st0, s.st1, s.st2, s.st3, s.st4, s.st5, s.st6, s.st7]
    todo, batch_of = ops[rank]
    open_stores, open_calls = set(), set()

    def dst(r):
        rid, pid = topo.addr(T.cores[r], core)
        return bass.DstId(rid=rid, pnc=pid)

    def release(k):
        if batch_of[k] in open_stores:
            g.wait_ge(st[batch_of[k]], 16)
            open_stores.discard(batch_of[k])
        if k in open_calls:
            g.wait_ge(snt[k], 8)
            open_calls.discard(k)

    signals = 0
    for step, order, what, arg in todo:
        if what == "recv":
            g.wait_ge(arr[arg], 8)
        elif what == "load":
            k, old = arg
            if old is not None:
                release(old)
            g.dma_start(T.slot[slot[rank][k]], T.x[k]).then_inc(s.ld, 16)
            g.wait_ge(s.ld, 16)
        elif what == "send":
            k = arg
            need = sum(1 for q in kids[k][rank] if k in credited[q])
            if need:
                g.wait_ge(cr[k], need)
            g.remote_dma_fused([bass.RemoteDMATransfer(
                dst_ids=[dst(q) for q in kids[k][rank]], dma_engine_mask=0xFF, remote_sem=arr[k],
                srcs=[T.slot[slot[rank][k]]], dsts=[T.slot[slot[q][k]] for q in kids[k][rank]])], local_sem=snt[k])
            open_calls.add(k)
        elif what == "store":
            i, ks = arg
            a, b = slot[rank][ks[0]], slot[rank][ks[-1]]
            if len(ks) == 1:
                g.dma_start(T.y[ks[0]], T.slot[a]).then_inc(st[i], 16)
            else:
                g.dma_start(T.y[ks[0]:ks[-1] + 1:ks[1] - ks[0]],
                            T.slot[a:b + 1:(b - a) // (len(ks) - 1)]).then_inc(st[i], 16)
            open_stores.add(i)
        else:
            for k, old in arg:
                release(old)
            g.remote_dma_fused([bass.RemoteDMATransfer(dst_ids=[dst(up[k][rank])], dma_engine_mask=1 << i, remote_sem=cr[k])
                                for i, (k, old) in enumerate(arg)], local_sem=s.sig)
            signals += len(arg)
    for k in range(ROUNDS):
        release(k)
    if signals:
        g.wait_ge(s.sig, signals)
